import numpy as np
import ml_dtypes


def mxq(x, axis, fmt="e4m3"):
    dtype, down = {"e4m3": (ml_dtypes.float8_e4m3fn, 7), "e5m2": (ml_dtypes.float8_e5m2, 14)}[fmt]
    v = np.moveaxis(np.asarray(x, np.float32).astype(ml_dtypes.bfloat16).astype(np.float64), axis, -1)
    blocks = v.reshape(v.shape[:-1] + (-1, 32))
    amax = np.abs(blocks).max(-1, keepdims=True)
    byte = np.maximum(np.where(amax > 0, np.frexp(amax)[1] - 1 + 127, 0) - down, 1)
    scale = np.exp2(byte - 127.0)
    codes = (blocks / scale).astype(np.float32).astype(dtype).astype(np.float64)
    return np.moveaxis((codes * scale).reshape(v.shape), -1, axis)


WIDE = False


def mx_kscale(k):
    if not WIDE:
        return np.ones(k)
    levels = np.array([10, -10, 5, -5, 0])
    if k % 512:
        return np.exp2(np.random.permutation(np.resize(levels, k // 32))).repeat(32)
    a = np.empty((k // 512, 16))
    for p in range(k // 512):
        a[p, :8] = np.random.permutation(np.resize(levels, 8))
        for g in range(8):
            far = levels[np.abs(levels - a[p, g]) >= 10]
            a[p, g + 8] = far[np.random.randint(len(far))]
    return np.exp2(a.ravel()).repeat(32)


def f64(x):
    return np.asarray(x).astype(np.float64)


def striped(idx):
    return np.tile(np.asarray(idx).reshape(-1, 16).T, (8, 1)).astype(np.uint16)


def unstriped(offs):
    return offs[:16].T.reshape(-1).astype(np.int64)


E2M1 = np.array([0.0, 0.5, 1.0, 1.5, 2.0, 3.0, 4.0, 6.0, -0.0, -0.5, -1.0, -1.5, -2.0, -3.0, -4.0, -6.0])


def pack_weight(w, fmt):
    k, n = w.shape
    w = f64(np.asarray(w, np.float32).astype(ml_dtypes.bfloat16)).reshape(k // 32, 32, n)
    amax = np.abs(w).max(1)
    if fmt == "e4m3":
        byte = np.frexp(amax)[1] - 1 + 127 - 7
    else:
        mant, ex = np.frexp(amax / 6.0)
        byte = np.where(mant > 0.5, ex, ex - 1) + 127
    byte = np.clip(np.where(amax > 0, byte, 1), 1, 254)
    scaled = (w * np.exp2(127.0 - byte)[:, None, :]).reshape(k, n).astype(np.float32)
    by_word = np.ascontiguousarray(scaled.reshape(k // 512, 128, 4, n).transpose(0, 1, 3, 2))
    if fmt == "e4m3":
        words = by_word.astype(ml_dtypes.float8_e4m3fn).view(np.uint8)
    else:
        c = by_word.astype(ml_dtypes.float4_e2m1fn).view(np.uint8) & 0xF
        words = (c[..., 0::2] | (c[..., 1::2] << 4)).reshape(k // 512, 128, 2 * n)
    return np.ascontiguousarray(words), np.ascontiguousarray(byte.astype(np.uint8).reshape(k // 512, 16, n))


def unpack_weight(words, scales, fmt):
    g, _, n = scales.shape
    words = np.ascontiguousarray(words).reshape(g, 128, n, -1)
    if fmt == "e4m3":
        vals = words.view(ml_dtypes.float8_e4m3fn).astype(np.float64)
    else:
        nib = np.empty((g, 128, n, 4), np.uint8)
        nib[..., 0::2] = words & 0xF
        nib[..., 1::2] = words >> 4
        vals = E2M1[nib]
    vals = vals * np.repeat(np.exp2(scales.astype(np.float64) - 127.0), 8, axis=1)[..., None]
    return vals.transpose(0, 1, 3, 2).reshape(g * 512, n)


B, N, T, D, DV, NQ = 1, 512, 2048, 512, 256, 128
CAP = 2.0


def setup_inputs():
    n = np.random.standard_normal
    idx = np.random.permutation(T)[:B * N]
    s = mx_kscale(D)[:, None]
    u = np.ones(T)
    u[idx] = mx_kscale(B * N)
    r = np.random.uniform(0.5, 2.0, T)
    k = n((D, T)) / s
    v = n((DV, T)) / (u * r)
    kp = pack_weight(k, "e4m3")
    return {
        "qT": (n((B, D, NQ)) * s * (0.80 / np.sqrt(D))).astype(np.float32),
        "k_words": kp[0],
        "k_scales": kp[1],
        "vT": v.astype(np.float32),
        "vs": np.tile(u * r, (128, 1)).astype(np.float32),
        "offs": striped(idx),
    }


def reference(qT, k_words, k_scales, vT, vs, offs):
    idx = unstriped(offs)
    k = unpack_weight(k_words, k_scales, "e4m3")
    v = f64(vT)
    pick = lambda x: x[:, idx].reshape(x.shape[0], B, N).transpose(1, 0, 2)
    q = f64(qT)
    score = mxq(q, 1, "e4m3").transpose(0, 2, 1) @ pick(k)
    score = CAP * np.tanh(score / CAP)
    p = np.square(np.maximum(score, 0.0))
    total = p.sum(-1, keepdims=True) + 1.0
    w = p * pick(f64(vs))[:, :1, :]
    y = mxq(w, 2, "e4m3") @ mxq(pick(v).transpose(0, 2, 1), 1, "e4m3")
    y = y / total
    return y

@@ -1,0 +1,137 @@
+from contextlib import ExitStack
+
+import concourse.mybir as mybir
+from concourse.masks import make_identity
+
+N, T, D, DV, NQ = 512, 2048, 512, 256, 128
+CAP = 2.0
+FLOPS = 2 * NQ * N * (D + DV)
+
+F32 = mybir.dt.float32
+BF16 = mybir.dt.bfloat16
+I32 = mybir.dt.int32
+U32 = mybir.dt.uint32
+U16 = mybir.dt.uint16
+U8 = mybir.dt.uint8
+FP8X4 = mybir.dt.float8_e4m3fn_x4
+ACT = mybir.ActivationFunctionType
+ALU = mybir.AluOpType
+
+P = 128
+PACK = 4
+VS_ROW = 8
+
+
+def dealt(ap):
+    return ap.rearrange("p (u h b j) -> p b u j h", u=2, h=2, b=16, j=8)
+
+
+def tile_attend_rel2_cap_topkq128n512t2048_kernel(tc, qT, k_words, k_scales, vT, vs, offs, out):
+    nc = tc.nc
+    with ExitStack() as ctx:
+        sb = ctx.enter_context(tc.tile_pool(name="sb", bufs=1))
+        ps = ctx.enter_context(tc.psum_pool(name="ps", bufs=1))
+
+        offsets = sb.tile([P, N // 16], U16, name="offsets")
+        nc.sync.dma_start(offsets[:], offs)
+
+        scale_pool = sb.tile([P, T], U8, name="scale_pool", tag="scales_then_v1", align_bytes=64)
+        nc.vector.memset(scale_pool[:].bitcast(I32), 0)
+
+        q_raw = sb.tile([P, PACK, NQ], F32, name="q_raw", tag="q_then_v", align_bytes=64)
+        nc.sync.dma_start(q_raw[:], qT[0].rearrange("(p t) q -> p t q", t=PACK))
+        for r in range(PACK):
+            nc.sync.dma_start(scale_pool[r:P:32, :].bitcast(I32), k_scales[0][r:16:4, :].bitcast(I32))
+
+        ident = sb.tile([P, P], F32, name="ident", align_bytes=64)
+        make_identity(nc, ident[:])
+        key_pool = sb.tile([P, T], U32, name="key_pool", tag="keys", align_bytes=64)
+        nc.sync.dma_start(key_pool[:].bitcast(I32), k_words[0].rearrange("p t r -> p (t r)").bitcast(I32))
+        vs_pool = sb.tile([P, T], F32, name="vs_pool", tag="vs_then_listed0", align_bytes=64)
+        nc.vector.memset(vs_pool[:], 0.0)
+        nc.scalar.dma_start(vs_pool[VS_ROW:VS_ROW + 1, :], vs[0:1, :])
+
+        q_bf = sb.tile([P, NQ, PACK], BF16, name="q_bf", align_bytes=64)
+        nc.vector.tensor_copy(q_bf[:], q_raw[:].rearrange("p t q -> p q t"))
+
+        v_pool0 = sb.tile([P, T], F32, name="v_pool0", tag="q_then_v", align_bytes=64)
+        nc.sync.dma_start(v_pool0[:], vT[0:P, :])
+
+        ks_listed = sb.tile([P, N], U8, name="ks_listed", tag="ks_then_codes", align_bytes=64)
+        nc.vector.tensor_copy(ks_listed[:], scale_pool[:].indirect(offsets[:]))
+        v_pool1 = sb.tile([P, T], F32, name="v_pool1", tag="scales_then_v1", align_bytes=64)
+        nc.sync.dma_start(v_pool1[:], vT[P:2 * P, :])
+        k_scale = sb.tile([P, N], U8, name="k_scale", align_bytes=64)
+        nc.vector.tensor_copy(dealt(k_scale[:]), ks_listed[:].rearrange("p (b u j h) -> p b u j h", b=16, u=2, j=8))
+
+        q_codes = sb.tile([P, NQ], U32, name="q_codes", align_bytes=64)
+        q_scale = sb.tile([P, NQ], U8, name="q_scale", align_bytes=64)
+        nc.vector.quantize_mx(out=q_codes[:].bitcast(FP8X4), scales=q_scale[:],
+                              in_=q_bf[:].rearrange("p q t -> p (q t)"))
+
+        k_codes = sb.tile([P, N], U32, name="k_codes", tag="ks_then_codes", align_bytes=64)
+        nc.vector.tensor_copy(dealt(k_codes[:]), key_pool[:].indirect(offsets[:]))
+
+        scores = ps.tile([P, PACK, NQ], F32, name="scores")
+        for r in range(PACK):
+            cols = slice(r * P, (r + 1) * P)
+            nc.tensor.matmul_mx(out=scores[:, r, :], lhsT=k_codes[:, cols].bitcast(FP8X4), lhsT_scale=k_scale[:, cols],
+                                rhs=q_codes[:].bitcast(FP8X4), rhs_scale=q_scale[:], start=True, stop=True)
+
+        vs_listed = sb.tile([P, N], F32, name="vs_listed", tag="keys", align_bytes=64)
+        nc.vector.tensor_copy(dealt(vs_listed[:].bitcast(U32)), vs_pool[:].bitcast(U32).indirect(offsets[:]))
+        vs_turned = ps.tile([P, PACK, P], F32, name="vs_turned")
+        for r in range(PACK):
+            nc.tensor.transpose(vs_turned[:, r, :], vs_listed[:, r * P:(r + 1) * P], ident[:])
+
+        tanh = sb.tile([P, NQ, PACK], F32, name="tanh", align_bytes=64)
+        nc.scalar.activation(tanh[:], scores[:].rearrange("p r q -> p q r"), ACT.Tanh, scale=1.0 / CAP)
+        positive = sb.tile([P, NQ, PACK], F32, name="positive", align_bytes=64)
+        nc.scalar.activation(positive[:], tanh[:], ACT.Relu, scale=CAP)
+        p = sb.tile([P, NQ, PACK], F32, name="p", align_bytes=64)
+        nc.scalar.activation(p[:], positive[:], ACT.Square)
+
+        def turn_values(pool, half, tag):
+            listed = sb.tile([P, N], BF16, name="v_listed%d" % half, tag=tag, align_bytes=64)
+            nc.vector.tensor_copy(listed[:].rearrange("p (u b c) -> p b u c", u=2, b=16), pool[:].indirect(offsets[:]))
+            words = listed[:].bitcast(F32)
+            turned = ps.tile([P, 2, P], F32, name="v_turned%d" % half)
+            for u in range(2):
+                nc.tensor.transpose(turned[:, u, :], words[:, u * P:(u + 1) * P], ident[:])
+            v_bf = sb.tile([P, P * PACK], BF16, name="v_bf%d" % half, align_bytes=64)
+            nc.scalar.copy(v_bf[:].bitcast(F32).rearrange("p (e u) -> p e u", u=2), turned[:].rearrange("p u e -> p e u"))
+            return v_bf
+
+        v_bf0 = turn_values(v_pool0, 0, "vs_then_listed0")
+
+        w = sb.tile([P, NQ, PACK], BF16, name="w", align_bytes=64)
+        nc.vector.tensor_tensor(w[:], p[:], vs_turned[:, :, VS_ROW].unsqueeze(1).to_broadcast([P, NQ, PACK]), ALU.mult)
+
+        p_tiles = sb.tile([P, PACK, NQ], F32, name="p_tiles", align_bytes=64)
+        nc.scalar.activation(p_tiles[:], positive[:].rearrange("p q r -> p r q"), ACT.Square)
+        p_turned = ps.tile([P, P], F32, name="p_turned")
+        for r in range(PACK):
+            nc.tensor.matmul(p_turned[:], p_tiles[:, r, :], ident[:], start=(r == 0), stop=(r == PACK - 1), is_transpose=True)
+        p_rows = sb.tile([P, P], F32, name="p_rows", align_bytes=64)
+        total = sb.tile([P, 1], F32, name="total")
+        nc.scalar.activation(p_rows[:], p_turned[:], ACT.Copy, bias=1.0 / P, accum_out=total[:])
+
+        v_bf1 = turn_values(v_pool1, 1, "listed1")
+
+        w_codes = sb.tile([P, NQ], U32, name="w_codes", align_bytes=64)
+        w_scale = sb.tile([P, NQ], U8, name="w_scale", align_bytes=64)
+        nc.vector.quantize_mx(out=w_codes[:].bitcast(FP8X4), scales=w_scale[:],
+                              in_=w[:].rearrange("p q t -> p (q t)"))
+        inv_total = sb.tile([P, 1], F32, name="inv_total")
+        nc.vector.reciprocal(inv_total[:], total[:])
+
+        for half, v_bf in enumerate((v_bf0, v_bf1)):
+            v_codes = sb.tile([P, P], U32, name="v_codes%d" % half, align_bytes=64)
+            v_scale = sb.tile([P, P], U8, name="v_scale%d" % half, align_bytes=64)
+            nc.vector.quantize_mx(out=v_codes[:].bitcast(FP8X4), scales=v_scale[:], in_=v_bf[:])
+            y = ps.tile([P, P], F32, name="y%d" % half)
+            nc.tensor.matmul_mx(out=y[:], lhsT=w_codes[:].bitcast(FP8X4), lhsT_scale=w_scale[:],
+                                rhs=v_codes[:].bitcast(FP8X4), rhs_scale=v_scale[:], start=True, stop=True)
+            result = sb.tile([P, P], F32, name="result%d" % half, align_bytes=64)
+            nc.scalar.activation(result[:], y[:], ACT.Copy, scale=inv_total[:])
+            nc.sync.dma_start(out[0][:, half * P:(half + 1) * P], result[:])

@@ -30,12 +30,13 @@ def tile_attend_rel2_cap_topkq128n512t2048_kernel(tc, qT, k_words, k_scales, vT,
     nc = tc.nc
     with ExitStack() as ctx:
         sb = ctx.enter_context(tc.tile_pool(name="sb", bufs=1))
+        reused = ctx.enter_context(tc.tile_pool(name="reused", bufs=1))
         ps = ctx.enter_context(tc.psum_pool(name="ps", bufs=1))
 
         offsets = sb.tile([P, N // 16], U16, name="offsets")
         nc.sync.dma_start(offsets[:], offs)
 
-        scale_pool = sb.tile([P, T], U8, name="scale_pool", tag="scales_then_v1", align_bytes=64)
+        scale_pool = reused.tile([P, T], U8, name="scale_pool", align_bytes=64, offset=0)
         nc.vector.memset(scale_pool[:].bitcast(I32), 0)
 
         q_raw = sb.tile([P, PACK, NQ], F32, name="q_raw", tag="q_then_v", align_bytes=64)
@@ -59,10 +60,11 @@ def tile_attend_rel2_cap_topkq128n512t2048_kernel(tc, qT, k_words, k_scales, vT,
 
         ks_listed = sb.tile([P, N], U8, name="ks_listed", tag="ks_then_codes", align_bytes=64)
         nc.vector.tensor_copy(ks_listed[:], scale_pool[:].indirect(offsets[:]))
-        v_pool1 = sb.tile([P, T], F32, name="v_pool1", tag="scales_then_v1", align_bytes=64)
+        v_pool1 = reused.tile([P, T], F32, name="v_pool1", align_bytes=64, offset=0)
         nc.sync.dma_start(v_pool1[:], vT[P:2 * P, :])
         k_scale = sb.tile([P, N], U8, name="k_scale", align_bytes=64)
-        nc.vector.tensor_copy(dealt(k_scale[:]), ks_listed[:].rearrange("p (b u j h) -> p b u j h", b=16, u=2, j=8))
+        nc.vector.tensor_copy(k_scale[:].rearrange("p (u h b j) -> p u h b j", u=2, h=2, b=16),
+                              ks_listed[:].rearrange("p (b u j h) -> p u h b j", b=16, u=2, j=8))
 
         q_codes = sb.tile([P, NQ], U32, name="q_codes", align_bytes=64)
         q_scale = sb.tile([P, NQ], U8, name="q_scale", align_bytes=64)
@@ -85,48 +87,54 @@ def tile_attend_rel2_cap_topkq128n512t2048_kernel(tc, qT, k_words, k_scales, vT,
             nc.tensor.transpose(vs_turned[:, r, :], vs_listed[:, r * P:(r + 1) * P], ident[:])
 
         tanh = sb.tile([P, NQ, PACK], F32, name="tanh", align_bytes=64)
-        nc.scalar.activation(tanh[:], scores[:].rearrange("p r q -> p q r"), ACT.Tanh, scale=1.0 / CAP)
-        positive = sb.tile([P, NQ, PACK], F32, name="positive", align_bytes=64)
-        nc.scalar.activation(positive[:], tanh[:], ACT.Relu, scale=CAP)
+        positive = sb.tile([P, NQ, PACK], F32, name="positive", tag="positive_then_v_bf0", align_bytes=64)
         p = sb.tile([P, NQ, PACK], F32, name="p", align_bytes=64)
-        nc.scalar.activation(p[:], positive[:], ACT.Square)
+        q_halves = (slice(0, NQ // 2), slice(NQ // 2, NQ))
+        for qs in q_halves:
+            nc.scalar.activation(tanh[:, qs, :], scores[:, :, qs].rearrange("p r q -> p q r"), ACT.Tanh, scale=1.0 / CAP)
+        for qs in q_halves:
+            nc.scalar.activation(positive[:, qs, :], tanh[:, qs, :], ACT.Relu, scale=CAP)
+        for qs in q_halves:
+            nc.scalar.activation(p[:, qs, :], positive[:, qs, :], ACT.Square)
 
-        def turn_values(pool, half, tag):
+        def turn_values(pool, half, tag, bf_tag):
             listed = sb.tile([P, N], BF16, name="v_listed%d" % half, tag=tag, align_bytes=64)
             nc.vector.tensor_copy(listed[:].rearrange("p (u b c) -> p b u c", u=2, b=16), pool[:].indirect(offsets[:]))
             words = listed[:].bitcast(F32)
             turned = ps.tile([P, 2, P], F32, name="v_turned%d" % half)
             for u in range(2):
                 nc.tensor.transpose(turned[:, u, :], words[:, u * P:(u + 1) * P], ident[:])
-            v_bf = sb.tile([P, P * PACK], BF16, name="v_bf%d" % half, align_bytes=64)
+            v_bf = sb.tile([P, P * PACK], BF16, name="v_bf%d" % half, tag=bf_tag, align_bytes=64)
             nc.scalar.copy(v_bf[:].bitcast(F32).rearrange("p (e u) -> p e u", u=2), turned[:].rearrange("p u e -> p e u"))
             return v_bf
 
-        v_bf0 = turn_values(v_pool0, 0, "vs_then_listed0")
+        v_bf0 = turn_values(v_pool0, 0, "vs_then_listed0", "positive_then_v_bf0")
+        vs_col = sb.tile([P, PACK], F32, name="vs_col", tag="q_then_v", align_bytes=64)
+        nc.vector.tensor_copy(vs_col[:], vs_turned[:, :, VS_ROW])
 
         w = sb.tile([P, NQ, PACK], BF16, name="w", align_bytes=64)
-        nc.vector.tensor_tensor(w[:], p[:], vs_turned[:, :, VS_ROW].unsqueeze(1).to_broadcast([P, NQ, PACK]), ALU.mult)
+        for qs in q_halves:
+            nc.vector.tensor_tensor(w[:, qs, :], p[:, qs, :],
+                                    vs_col[:].unsqueeze(1).to_broadcast([P, NQ // 2, PACK]), ALU.mult)
 
-        p_tiles = sb.tile([P, PACK, NQ], F32, name="p_tiles", align_bytes=64)
-        nc.scalar.activation(p_tiles[:], positive[:].rearrange("p q r -> p r q"), ACT.Square)
         p_turned = ps.tile([P, P], F32, name="p_turned")
         for r in range(PACK):
-            nc.tensor.matmul(p_turned[:], p_tiles[:, r, :], ident[:], start=(r == 0), stop=(r == PACK - 1), is_transpose=True)
+            nc.tensor.matmul(p_turned[:], p[:, :, r], ident[:], start=(r == 0), stop=(r == PACK - 1), is_transpose=True)
         p_rows = sb.tile([P, P], F32, name="p_rows", align_bytes=64)
         total = sb.tile([P, 1], F32, name="total")
         nc.scalar.activation(p_rows[:], p_turned[:], ACT.Copy, bias=1.0 / P, accum_out=total[:])
 
-        v_bf1 = turn_values(v_pool1, 1, "listed1")
+        v_bf1 = turn_values(v_pool1, 1, "q_then_v", "v_bf1")
 
-        w_codes = sb.tile([P, NQ], U32, name="w_codes", align_bytes=64)
+        w_codes = reused.tile([P, NQ], U32, name="w_codes", align_bytes=64, offset=0)
         w_scale = sb.tile([P, NQ], U8, name="w_scale", align_bytes=64)
         nc.vector.quantize_mx(out=w_codes[:].bitcast(FP8X4), scales=w_scale[:],
                               in_=w[:].rearrange("p q t -> p (q t)"))
-        inv_total = sb.tile([P, 1], F32, name="inv_total")
+        inv_total = reused.tile([P, 1], F32, name="inv_total", align_bytes=64, offset=512)
         nc.vector.reciprocal(inv_total[:], total[:])
 
         for half, v_bf in enumerate((v_bf0, v_bf1)):
-            v_codes = sb.tile([P, P], U32, name="v_codes%d" % half, align_bytes=64)
+            v_codes = reused.tile([P, P], U32, name="v_codes%d" % half, align_bytes=64, offset=1024 + 512 * half)
             v_scale = sb.tile([P, P], U8, name="v_scale%d" % half, align_bytes=64)
             nc.vector.quantize_mx(out=v_codes[:].bitcast(FP8X4), scales=v_scale[:], in_=v_bf[:])
             y = ps.tile([P, P], F32, name="y%d" % half)

@@ -48,17 +48,17 @@ def tile_attend_rel2_cap_topkq128n512t2048_kernel(tc, qT, k_words, k_scales, vT,
         make_identity(nc, ident[:])
         key_pool = sb.tile([P, T], U32, name="key_pool", tag="keys", align_bytes=64)
         nc.sync.dma_start(key_pool[:].bitcast(I32), k_words[0].rearrange("p t r -> p (t r)").bitcast(I32))
-        vs_pool = sb.tile([P, T], F32, name="vs_pool", tag="vs_then_listed0", align_bytes=64)
+        vs_pool = sb.tile([P, T], F32, name="vs_pool", align_bytes=64)
         nc.vector.memset(vs_pool[:], 0.0)
         nc.scalar.dma_start(vs_pool[VS_ROW:VS_ROW + 1, :], vs[0:1, :])
 
         q_bf = sb.tile([P, NQ, PACK], BF16, name="q_bf", align_bytes=64)
         nc.vector.tensor_copy(q_bf[:], q_raw[:].rearrange("p t q -> p q t"))
-
         v_pool0 = sb.tile([P, T], F32, name="v_pool0", tag="q_then_v", align_bytes=64)
         nc.sync.dma_start(v_pool0[:], vT[0:P, :])
 
-        ks_listed = sb.tile([P, N], U8, name="ks_listed", tag="ks_then_codes", align_bytes=64)
+
+        ks_listed = sb.tile([P, N], U8, name="ks_listed", align_bytes=64)
         nc.vector.tensor_copy(ks_listed[:], scale_pool[:].indirect(offsets[:]))
         v_pool1 = reused.tile([P, T], F32, name="v_pool1", align_bytes=64, offset=0)
         nc.sync.dma_start(v_pool1[:], vT[P:2 * P, :])
@@ -71,7 +71,7 @@ def tile_attend_rel2_cap_topkq128n512t2048_kernel(tc, qT, k_words, k_scales, vT,
         nc.vector.quantize_mx(out=q_codes[:].bitcast(FP8X4), scales=q_scale[:],
                               in_=q_bf[:].rearrange("p q t -> p (q t)"))
 
-        k_codes = sb.tile([P, N], U32, name="k_codes", tag="ks_then_codes", align_bytes=64)
+        k_codes = sb.tile([P, N], U32, name="k_codes", align_bytes=64)
         nc.vector.tensor_copy(dealt(k_codes[:]), key_pool[:].indirect(offsets[:]))
 
         scores = ps.tile([P, PACK, NQ], F32, name="scores")
@@ -87,7 +87,7 @@ def tile_attend_rel2_cap_topkq128n512t2048_kernel(tc, qT, k_words, k_scales, vT,
             nc.tensor.transpose(vs_turned[:, r, :], vs_listed[:, r * P:(r + 1) * P], ident[:])
 
         tanh = sb.tile([P, NQ, PACK], F32, name="tanh", align_bytes=64)
-        positive = sb.tile([P, NQ, PACK], F32, name="positive", tag="positive_then_v_bf0", align_bytes=64)
+        positive = sb.tile([P, NQ, PACK], F32, name="positive", align_bytes=64)
         p = sb.tile([P, NQ, PACK], F32, name="p", align_bytes=64)
         q_halves = (slice(0, NQ // 2), slice(NQ // 2, NQ))
         for qs in q_halves:
@@ -97,44 +97,46 @@ def tile_attend_rel2_cap_topkq128n512t2048_kernel(tc, qT, k_words, k_scales, vT,
         for qs in q_halves:
             nc.scalar.activation(p[:, qs, :], positive[:, qs, :], ACT.Square)
 
-        def turn_values(pool, half, tag, bf_tag):
-            listed = sb.tile([P, N], BF16, name="v_listed%d" % half, tag=tag, align_bytes=64)
+        def turn_values(pool, half, turned):
+            listed = sb.tile([P, N], BF16, name="v_listed%d" % half, align_bytes=64)
             nc.vector.tensor_copy(listed[:].rearrange("p (u b c) -> p b u c", u=2, b=16), pool[:].indirect(offsets[:]))
             words = listed[:].bitcast(F32)
-            turned = ps.tile([P, 2, P], F32, name="v_turned%d" % half)
             for u in range(2):
                 nc.tensor.transpose(turned[:, u, :], words[:, u * P:(u + 1) * P], ident[:])
-            v_bf = sb.tile([P, P * PACK], BF16, name="v_bf%d" % half, tag=bf_tag, align_bytes=64)
-            nc.scalar.copy(v_bf[:].bitcast(F32).rearrange("p (e u) -> p e u", u=2), turned[:].rearrange("p u e -> p e u"))
+
+        def weave_values(turned, half, tag):
+            v_bf = sb.tile([P, P * PACK], BF16, name="v_bf%d" % half, tag=tag, align_bytes=64)
+            nc.scalar.copy(v_bf[:].bitcast(F32).rearrange("p (e u) -> p e u", u=2), turned.rearrange("p u e -> p e u"))
             return v_bf
 
-        v_bf0 = turn_values(v_pool0, 0, "vs_then_listed0", "positive_then_v_bf0")
-        vs_col = sb.tile([P, PACK], F32, name="vs_col", tag="q_then_v", align_bytes=64)
-        nc.vector.tensor_copy(vs_col[:], vs_turned[:, :, VS_ROW])
-
-        w = sb.tile([P, NQ, PACK], BF16, name="w", align_bytes=64)
-        for qs in q_halves:
-            nc.vector.tensor_tensor(w[:, qs, :], p[:, qs, :],
-                                    vs_col[:].unsqueeze(1).to_broadcast([P, NQ // 2, PACK]), ALU.mult)
-
-        p_turned = ps.tile([P, P], F32, name="p_turned")
+        shared_bank = ps.tile([P, 3, P], F32, name="shared_bank")
+        turn_values(v_pool0, 0, shared_bank[:, 0:2, :])
+        p_turned = shared_bank[:, 2, :]
         for r in range(PACK):
-            nc.tensor.matmul(p_turned[:], p[:, :, r], ident[:], start=(r == 0), stop=(r == PACK - 1), is_transpose=True)
+            nc.tensor.matmul(p_turned, p[:, :, r], ident[:], start=(r == 0), stop=(r == PACK - 1), is_transpose=True)
+        v_bf0 = weave_values(shared_bank[:, 0:2, :], 0, "v_bf0")
         p_rows = sb.tile([P, P], F32, name="p_rows", align_bytes=64)
         total = sb.tile([P, 1], F32, name="total")
-        nc.scalar.activation(p_rows[:], p_turned[:], ACT.Copy, bias=1.0 / P, accum_out=total[:])
+        nc.scalar.activation(p_rows[:], p_turned, ACT.Copy, bias=1.0 / P, accum_out=total[:])
 
-        v_bf1 = turn_values(v_pool1, 1, "q_then_v", "v_bf1")
+        v_turned1 = ps.tile([P, 2, P], F32, name="v_turned1")
+        turn_values(v_pool1, 1, v_turned1[:])
+        v_bf1 = weave_values(v_turned1[:], 1, "v_bf1")
 
-        w_codes = reused.tile([P, NQ], U32, name="w_codes", align_bytes=64, offset=0)
+        w = reused.tile([P, NQ, PACK], BF16, name="w", align_bytes=64, offset=0)
+        for qs in q_halves:
+            nc.vector.tensor_tensor(w[:, qs, :], p[:, qs, :],
+                                    vs_turned[:, :, VS_ROW].unsqueeze(1).to_broadcast([P, NQ // 2, PACK]), ALU.mult)
+
+        w_codes = sb.tile([P, NQ], U32, name="w_codes", align_bytes=64)
         w_scale = sb.tile([P, NQ], U8, name="w_scale", align_bytes=64)
         nc.vector.quantize_mx(out=w_codes[:].bitcast(FP8X4), scales=w_scale[:],
                               in_=w[:].rearrange("p q t -> p (q t)"))
-        inv_total = reused.tile([P, 1], F32, name="inv_total", align_bytes=64, offset=512)
+        inv_total = reused.tile([P, 1], F32, name="inv_total", align_bytes=64, offset=1024)
         nc.vector.reciprocal(inv_total[:], total[:])
 
         for half, v_bf in enumerate((v_bf0, v_bf1)):
-            v_codes = reused.tile([P, P], U32, name="v_codes%d" % half, align_bytes=64, offset=1024 + 512 * half)
+            v_codes = reused.tile([P, P], U32, name="v_codes%d" % half, align_bytes=64, offset=2048 + 512 * half)
             v_scale = sb.tile([P, P], U8, name="v_scale%d" % half, align_bytes=64)
             nc.vector.quantize_mx(out=v_codes[:].bitcast(FP8X4), scales=v_scale[:], in_=v_bf[:])
             y = ps.tile([P, P], F32, name="y%d" % half)

from contextlib import ExitStack

import concourse.mybir as mybir
from concourse.masks import make_identity

N, T, D, DV, NQ = 512, 2048, 512, 256, 128
CAP = 2.0
FLOPS = 2 * NQ * N * (D + DV)

F32 = mybir.dt.float32
BF16 = mybir.dt.bfloat16
I32 = mybir.dt.int32
U32 = mybir.dt.uint32
U16 = mybir.dt.uint16
U8 = mybir.dt.uint8
FP8X4 = mybir.dt.float8_e4m3fn_x4
ACT = mybir.ActivationFunctionType
ALU = mybir.AluOpType

P = 128
PACK = 4
VS_ROW = 8


def dealt(ap):
    return ap.rearrange("p (u h b j) -> p b u j h", u=2, h=2, b=16, j=8)


def tile_attend_rel2_cap_topkq128n512t2048_kernel(tc, qT, k_words, k_scales, vT, vs, offs, out):
    nc = tc.nc
    with ExitStack() as ctx:
        sb = ctx.enter_context(tc.tile_pool(name="sb", bufs=1))
        reused = ctx.enter_context(tc.tile_pool(name="reused", bufs=1))
        ps = ctx.enter_context(tc.psum_pool(name="ps", bufs=1))

        offsets = sb.tile([P, N // 16], U16, name="offsets")
        nc.sync.dma_start(offsets[:], offs)

        scale_pool = reused.tile([P, T], U8, name="scale_pool", align_bytes=64, offset=0)
        nc.vector.memset(scale_pool[:].bitcast(I32), 0)

        q_raw = sb.tile([P, PACK, NQ], F32, name="q_raw", tag="q_then_v", align_bytes=64)
        nc.sync.dma_start(q_raw[:], qT[0].rearrange("(p t) q -> p t q", t=PACK))
        for r in range(PACK):
            nc.sync.dma_start(scale_pool[r:P:32, :].bitcast(I32), k_scales[0][r:16:4, :].bitcast(I32))

        ident = sb.tile([P, P], F32, name="ident", align_bytes=64)
        make_identity(nc, ident[:])
        key_pool = sb.tile([P, T], U32, name="key_pool", tag="keys", align_bytes=64)
        nc.sync.dma_start(key_pool[:].bitcast(I32), k_words[0].rearrange("p t r -> p (t r)").bitcast(I32))
        vs_pool = sb.tile([P, T], F32, name="vs_pool", align_bytes=64)
        nc.vector.memset(vs_pool[:], 0.0)
        nc.scalar.dma_start(vs_pool[VS_ROW:VS_ROW + 1, :], vs[0:1, :])

        q_bf = sb.tile([P, NQ, PACK], BF16, name="q_bf", align_bytes=64)
        nc.vector.tensor_copy(q_bf[:], q_raw[:].rearrange("p t q -> p q t"))
        v_pool0 = sb.tile([P, T], F32, name="v_pool0", tag="q_then_v", align_bytes=64)
        nc.sync.dma_start(v_pool0[:], vT[0:P, :])


        ks_listed = sb.tile([P, N], U8, name="ks_listed", align_bytes=64)
        nc.vector.tensor_copy(ks_listed[:], scale_pool[:].indirect(offsets[:]))
        v_pool1 = reused.tile([P, T], F32, name="v_pool1", align_bytes=64, offset=0)
        nc.sync.dma_start(v_pool1[:], vT[P:2 * P, :])
        k_scale = sb.tile([P, N], U8, name="k_scale", align_bytes=64)
        nc.vector.tensor_copy(k_scale[:].rearrange("p (u h b j) -> p u h b j", u=2, h=2, b=16),
                              ks_listed[:].rearrange("p (b u j h) -> p u h b j", b=16, u=2, j=8))

        q_codes = sb.tile([P, NQ], U32, name="q_codes", align_bytes=64)
        q_scale = sb.tile([P, NQ], U8, name="q_scale", align_bytes=64)
        nc.vector.quantize_mx(out=q_codes[:].bitcast(FP8X4), scales=q_scale[:],
                              in_=q_bf[:].rearrange("p q t -> p (q t)"))

        k_codes = sb.tile([P, N], U32, name="k_codes", align_bytes=64)
        nc.vector.tensor_copy(dealt(k_codes[:]), key_pool[:].indirect(offsets[:]))

        scores = ps.tile([P, PACK, NQ], F32, name="scores")
        for r in range(PACK):
            cols = slice(r * P, (r + 1) * P)
            nc.tensor.matmul_mx(out=scores[:, r, :], lhsT=k_codes[:, cols].bitcast(FP8X4), lhsT_scale=k_scale[:, cols],
                                rhs=q_codes[:].bitcast(FP8X4), rhs_scale=q_scale[:], start=True, stop=True)

        vs_listed = sb.tile([P, N], F32, name="vs_listed", tag="keys", align_bytes=64)
        nc.vector.tensor_copy(dealt(vs_listed[:].bitcast(U32)), vs_pool[:].bitcast(U32).indirect(offsets[:]))
        vs_turned = ps.tile([P, PACK, P], F32, name="vs_turned")
        for r in range(PACK):
            nc.tensor.transpose(vs_turned[:, r, :], vs_listed[:, r * P:(r + 1) * P], ident[:])

        tanh = sb.tile([P, NQ, PACK], F32, name="tanh", align_bytes=64)
        positive = sb.tile([P, NQ, PACK], F32, name="positive", align_bytes=64)
        p = sb.tile([P, NQ, PACK], F32, name="p", align_bytes=64)
        q_halves = (slice(0, NQ // 2), slice(NQ // 2, NQ))
        for qs in q_halves:
            nc.scalar.activation(tanh[:, qs, :], scores[:, :, qs].rearrange("p r q -> p q r"), ACT.Tanh, scale=1.0 / CAP)
        for qs in q_halves:
            nc.scalar.activation(positive[:, qs, :], tanh[:, qs, :], ACT.Relu, scale=CAP)
        for qs in q_halves:
            nc.scalar.activation(p[:, qs, :], positive[:, qs, :], ACT.Square)

        def turn_values(pool, half, turned):
            listed = sb.tile([P, N], BF16, name="v_listed%d" % half, align_bytes=64)
            nc.vector.tensor_copy(listed[:].rearrange("p (u b c) -> p b u c", u=2, b=16), pool[:].indirect(offsets[:]))
            words = listed[:].bitcast(F32)
            for u in range(2):
                nc.tensor.transpose(turned[:, u, :], words[:, u * P:(u + 1) * P], ident[:])

        def weave_values(turned, half, tag):
            v_bf = sb.tile([P, P * PACK], BF16, name="v_bf%d" % half, tag=tag, align_bytes=64)
            nc.scalar.copy(v_bf[:].bitcast(F32).rearrange("p (e u) -> p e u", u=2), turned.rearrange("p u e -> p e u"))
            return v_bf

        shared_bank = ps.tile([P, 3, P], F32, name="shared_bank")
        turn_values(v_pool0, 0, shared_bank[:, 0:2, :])
        p_turned = shared_bank[:, 2, :]
        for r in range(PACK):
            nc.tensor.matmul(p_turned, p[:, :, r], ident[:], start=(r == 0), stop=(r == PACK - 1), is_transpose=True)
        v_bf0 = weave_values(shared_bank[:, 0:2, :], 0, "v_bf0")
        p_rows = sb.tile([P, P], F32, name="p_rows", align_bytes=64)
        total = sb.tile([P, 1], F32, name="total")
        nc.scalar.activation(p_rows[:], p_turned, ACT.Copy, bias=1.0 / P, accum_out=total[:])

        v_turned1 = ps.tile([P, 2, P], F32, name="v_turned1")
        turn_values(v_pool1, 1, v_turned1[:])
        v_bf1 = weave_values(v_turned1[:], 1, "v_bf1")

        w = reused.tile([P, NQ, PACK], BF16, name="w", align_bytes=64, offset=0)
        for qs in q_halves:
            nc.vector.tensor_tensor(w[:, qs, :], p[:, qs, :],
                                    vs_turned[:, :, VS_ROW].unsqueeze(1).to_broadcast([P, NQ // 2, PACK]), ALU.mult)

        w_codes = sb.tile([P, NQ], U32, name="w_codes", align_bytes=64)
        w_scale = sb.tile([P, NQ], U8, name="w_scale", align_bytes=64)
        nc.vector.quantize_mx(out=w_codes[:].bitcast(FP8X4), scales=w_scale[:],
                              in_=w[:].rearrange("p q t -> p (q t)"))
        inv_total = reused.tile([P, 1], F32, name="inv_total", align_bytes=64, offset=1024)
        nc.vector.reciprocal(inv_total[:], total[:])

        for half, v_bf in enumerate((v_bf0, v_bf1)):
            v_codes = reused.tile([P, P], U32, name="v_codes%d" % half, align_bytes=64, offset=2048 + 512 * half)
            v_scale = sb.tile([P, P], U8, name="v_scale%d" % half, align_bytes=64)
            nc.vector.quantize_mx(out=v_codes[:].bitcast(FP8X4), scales=v_scale[:], in_=v_bf[:])
            y = ps.tile([P, P], F32, name="y%d" % half)
            nc.tensor.matmul_mx(out=y[:], lhsT=w_codes[:].bitcast(FP8X4), lhsT_scale=w_scale[:],
                                rhs=v_codes[:].bitcast(FP8X4), rhs_scale=v_scale[:], start=True, stop=True)
            result = sb.tile([P, P], F32, name="result%d" % half, align_bytes=64)
            nc.scalar.activation(result[:], y[:], ACT.Copy, scale=inv_total[:])
            nc.sync.dma_start(out[0][:, half * P:(half + 1) * P], result[:])
